import numpy as np
import ml_dtypes


def mxq(x, axis, fmt="e4m3"):
    dtype, down = {"e4m3": (ml_dtypes.float8_e4m3fn, 7), "e5m2": (ml_dtypes.float8_e5m2, 14)}[fmt]
    v = np.moveaxis(np.asarray(x, np.float32).astype(ml_dtypes.bfloat16).astype(np.float64), axis, -1)
    blocks = v.reshape(v.shape[:-1] + (-1, 32))
    amax = np.abs(blocks).max(-1, keepdims=True)
    byte = np.maximum(np.where(amax > 0, np.frexp(amax)[1] - 1 + 127, 0) - down, 1)
    scale = np.exp2(byte - 127.0)
    codes = (blocks / scale).astype(np.float32).astype(dtype).astype(np.float64)
    return np.moveaxis((codes * scale).reshape(v.shape), -1, axis)


WIDE = False


def mx_kscale(k):
    if not WIDE:
        return np.ones(k)
    levels = np.array([10, -10, 5, -5, 0])
    if k % 512:
        return np.exp2(np.random.permutation(np.resize(levels, k // 32))).repeat(32)
    a = np.empty((k // 512, 16))
    for p in range(k // 512):
        a[p, :8] = np.random.permutation(np.resize(levels, 8))
        for g in range(8):
            far = levels[np.abs(levels - a[p, g]) >= 10]
            a[p, g + 8] = far[np.random.randint(len(far))]
    return np.exp2(a.ravel()).repeat(32)


def f64(x):
    return np.asarray(x).astype(np.float64)


def striped(idx):
    return np.tile(idx.reshape(-1, 16).T, (8, 1)).astype(np.uint16)


def unstriped(offs):
    return offs[:16].T.reshape(-1).astype(np.int64)


def pack_weight(w):
    k, n = w.shape
    w = f64(np.asarray(w, np.float32).astype(ml_dtypes.bfloat16)).reshape(k // 32, 32, n)
    amax = np.abs(w).max(1)
    byte = np.clip(np.where(amax > 0, np.frexp(amax)[1] - 1 + 127 - 7, 1), 1, 254)
    scaled = (w * np.exp2(127.0 - byte)[:, None, :]).reshape(k, n).astype(np.float32)
    words = np.ascontiguousarray(scaled.reshape(k // 512, 128, 4, n).transpose(0, 1, 3, 2)).astype(ml_dtypes.float8_e4m3fn).view(np.uint8)
    return words, np.ascontiguousarray(byte.astype(np.uint8).reshape(k // 512, 16, n))


def unpack_weight(words, scales):
    g, p, n, _ = words.shape
    vals = np.ascontiguousarray(words).view(ml_dtypes.float8_e4m3fn).astype(np.float64) * np.repeat(np.exp2(scales.astype(np.float64) - 127.0), 8, axis=1)[..., None]
    return vals.transpose(0, 1, 3, 2).reshape(g * 512, n)


K, T, S, N, H = 1024, 2048, 512, 256, 512


def setup_inputs():
    n = np.random.standard_normal
    s = mx_kscale(K)[:, None]
    u = mx_kscale(H)
    packed_xT = pack_weight(n((K, T)) * s)
    return {
        "x_words": packed_xT[0],
        "x_scales": packed_xT[1],
        "w1": (n((K, H)) / np.sqrt(K) / s).astype(np.float32),
        "unit": (np.random.uniform(0.6, 1.4, (H, 1)) * u[:, None]).astype(np.float32),
        "w2": (n((H, N)) / np.sqrt(H) / u[:, None]).astype(np.float32),
        "offs": striped(np.random.permutation(T)[:S]),
        "d1": striped(np.random.permutation(S)),
        "d2": striped(np.random.permutation(S)),
    }


def reference(x_words, x_scales, w1, unit, w2, offs, d1, d2):
    xq = unpack_weight(x_words, x_scales)[:, unstriped(offs)]
    y = mxq(f64(w1), 0, "e4m3").T @ xq
    s1 = y[:, unstriped(d1)]
    ad = y * s1
    st = ad + ad[:, unstriped(d2)]
    ex = np.exp(1.5 * np.tanh(st))
    pr = ex / ex.mean(axis=1, keepdims=True)
    hid = f64(unit) * (pr * y)
    return mxq(f64(w2), 0, "e4m3").T @ mxq(hid, 0, "e4m3")

@@ -1,0 +1,213 @@
+from contextlib import ExitStack
+
+import concourse.mybir as mybir
+
+K, T, S, N, H = 1024, 2048, 512, 256, 512
+FLOPS = 2 * K * H * S + 2 * H * N * S
+
+F32 = mybir.dt.float32
+BF16 = mybir.dt.bfloat16
+I32 = mybir.dt.int32
+U32 = mybir.dt.uint32
+U16 = mybir.dt.uint16
+U8 = mybir.dt.uint8
+FP8X4 = mybir.dt.float8_e4m3fn_x4
+MULT = mybir.AluOpType.mult
+ADD = mybir.AluOpType.add
+ACT = mybir.ActivationFunctionType
+
+P = 128
+PACK = 4
+PASSES = K // (P * PACK)
+WIN = 704
+HALF = S // 2
+W1_CHUNKS = [(0, 256, "S"), (256, 512, "V")]
+ENG_A = "VSVS"
+ENG_B = "SVSV"
+ENG_C = "VVVV"
+ENG_D = "SSVS"
+ENG_E = "VVVV"
+
+
+def tile_picked_yanti_val_p_kernel(tc, x_words, x_scales, w1, unit, w2, offs, d1, d2, out):
+    nc = tc.nc
+    with ExitStack() as ctx:
+        lists = ctx.enter_context(tc.tile_pool(name="lists", bufs=1))
+        keep = ctx.enter_context(tc.tile_pool(name="keep", bufs=1))
+        psum = ctx.enter_context(tc.psum_pool(name="psum", bufs=1))
+
+        offs_sb = lists.tile([P, S // 16], U16, name="offs_sb")
+        d1_sb = lists.tile([P, S // 16], U16, name="d1_sb")
+        d2_sb = lists.tile([P, S // 16], U16, name="d2_sb")
+
+        xs_all = keep.tile([P, T], U8, name="xs_all", align_bytes=64)
+        nc.gpsimd.memset(xs_all[:].bitcast(I32), 0)
+        y_sb = [keep.tile([P, WIN], F32, name="y_sb%d" % t, align_bytes=64) for t in range(PACK)]
+        ad_sb = [keep.tile([P, WIN], F32, name="ad_sb%d" % t, align_bytes=64) for t in range(PACK)]
+        for t in range(PACK):
+            nc.vector.memset(y_sb[t][:, S:WIN], 0.0)
+            nc.vector.memset(ad_sb[t][:, S:WIN], 0.0)
+
+        nc.sync.dma_start(offs_sb[:], offs)
+        xs_i32 = x_scales.bitcast(I32)
+        for q in range(4):
+            nc.gpsimd.dma_start(out=xs_all[32 * q : 32 * q + 8, :].bitcast(I32), in_=xs_i32[:, 4 * q : 4 * q + 4, :])
+        w1_raw = {}
+        xw_all = []
+        w1_rows = w1.rearrange("(g p j) c -> g p j c", g=PASSES, j=PACK)
+
+        def load_w1(g, c0, c1):
+            raw = keep.tile([P, PACK, c1 - c0], F32, name="w1_raw%d_%d" % (g, c0), align_bytes=64)
+            nc.sync.dma_start(out=raw[:], in_=w1_rows[g, :, :, c0:c1])
+            w1_raw[(g, c0)] = raw
+
+        def load_x(g):
+            xw = keep.tile([P, T], I32, name="xw_all%d" % g, align_bytes=64)
+            nc.sync.dma_start(out=xw[:], in_=x_words[g].rearrange("p n r -> p (n r)").bitcast(I32))
+            xw_all.append(xw)
+
+        load_w1(0, 0, H)
+        load_x(0)
+        load_x(1)
+        for c0, c1, e in W1_CHUNKS:
+            load_w1(1, c0, c1)
+        nc.sync.dma_start(d1_sb[:], d1)
+        nc.sync.dma_start(d2_sb[:], d2)
+        unit_sb = keep.tile([P, PACK], F32, name="unit_sb", align_bytes=64)
+        nc.sync.dma_start(out=unit_sb[:], in_=unit.rearrange("(p t) o -> p (t o)", t=PACK))
+        w2_raw = keep.tile([P, PACK, N], F32, name="w2_raw", align_bytes=64)
+        nc.sync.dma_start(out=w2_raw[:], in_=w2.rearrange("(p j) n -> p j n", j=PACK))
+
+        xs = keep.tile([P, S], U8, name="xs", align_bytes=64)
+        nc.vector.tensor_copy(xs[:], xs_all[:].indirect(offs_sb[:]))
+        xw = [keep.tile([P, S], U32, name="xw%d" % g, align_bytes=64) for g in range(PASSES)]
+
+        w1_bf = [keep.tile([P, PACK, P, PACK], BF16, name="w1_bf%d" % g, align_bytes=64) for g in range(PASSES)]
+        w1_codes = [keep.tile([P, H], U32, name="w1_codes%d" % g, align_bytes=64) for g in range(PASSES)]
+        w1_scales = [keep.tile([P, H], U8, name="w1_scales%d" % g, align_bytes=64) for g in range(PASSES)]
+
+        def copy_on(e, dst, src):
+            if e == "S":
+                nc.scalar.copy(dst, src)
+            elif e == "G":
+                nc.gpsimd.tensor_copy(dst, src)
+            else:
+                nc.vector.tensor_copy(dst, src)
+
+        def cast_w1(g, c0, c1, e):
+            dst = w1_bf[g][:, :, c0 // PACK : c1 // PACK, :].rearrange("p t m j -> p m j t")
+            src = w1_raw[(g, c0)][:].rearrange("p j (m t) -> p m j t", t=PACK)
+            copy_on(e, dst, src)
+
+        def quant_w1(g, t0, t1):
+            nc.vector.quantize_mx(
+                out=w1_codes[g][:, t0 * P : t1 * P].bitcast(FP8X4),
+                scales=w1_scales[g][:, t0 * P : t1 * P],
+                in_=w1_bf[g][:, t0:t1].rearrange("p t m j -> p (t m j)"),
+            )
+
+        y_ps = [psum.tile([P, S], F32, name="y_ps%d" % t) for t in range(PACK)]
+
+        def mm1(g, t):
+            nc.tensor.matmul_mx(
+                out=y_ps[t][:],
+                lhsT=w1_codes[g][:, t * P : (t + 1) * P].bitcast(FP8X4),
+                lhsT_scale=w1_scales[g][:, t * P : (t + 1) * P],
+                rhs=xw[g][:].bitcast(FP8X4),
+                rhs_scale=xs[4 * g : P, :],
+                start=(g == 0),
+                stop=(g == PASSES - 1),
+            )
+
+        cast_w1(0, 0, H, "S")
+        quant_w1(0, 0, PACK)
+        nc.vector.tensor_copy(xw[0][:], xw_all[0][:].bitcast(U32).indirect(offs_sb[:]))
+        for t in range(PACK):
+            mm1(0, t)
+        nc.vector.tensor_copy(xw[1][:], xw_all[1][:].bitcast(U32).indirect(offs_sb[:]))
+        for c0, c1, e in W1_CHUNKS:
+            cast_w1(1, c0, c1, e)
+        for t in range(PACK):
+            quant_w1(1, t, t + 1)
+            mm1(1, t)
+
+        unit_s = keep.tile([P, PACK], F32, name="unit_s", align_bytes=64)
+        nc.vector.tensor_scalar(unit_s[:], unit_sb[:], float(S), None, MULT)
+
+        def gather_on(e, dst, window):
+            if e == "S":
+                nc.scalar.activation(dst, window, ACT.Copy)
+            else:
+                nc.vector.tensor_copy(dst, window)
+
+        s1 = [keep.tile([P, S], F32, name="s1_%d" % t, align_bytes=64) for t in range(PACK)]
+        s2 = [keep.tile([P, S], F32, name="s2_%d" % t, align_bytes=64) for t in range(PACK)]
+        st = [keep.tile([P, S], F32, name="st%d" % t, align_bytes=64) for t in range(PACK)]
+        th = [keep.tile([P, S], F32, name="th%d" % t, align_bytes=64) for t in range(PACK)]
+        ex = [keep.tile([P, S], F32, name="ex%d" % t, align_bytes=64) for t in range(PACK)]
+        tot = [keep.tile([P, 1], F32, name="tot%d" % t, align_bytes=64) for t in range(PACK)]
+        inv = [keep.tile([P, 1], F32, name="inv%d" % t, align_bytes=64) for t in range(PACK)]
+        fac = [keep.tile([P, 1], F32, name="fac%d" % t, align_bytes=64) for t in range(PACK)]
+        hid_pl = [keep.tile([P, PACK, HALF], BF16, name="hid_pl%d" % h, align_bytes=64) for h in range(2)]
+
+        def step(i, t):
+            if i == 0:
+                copy_on(ENG_A[t], y_sb[t][:, 0:S], y_ps[t][:])
+            elif i == 1:
+                gather_on(ENG_B[t], s1[t][:], y_sb[t][:].indirect(d1_sb[:]))
+            elif i == 2:
+                if ENG_C[t] == "G":
+                    nc.gpsimd.tensor_tensor(ad_sb[t][:, 0:S], s1[t][:], y_sb[t][:, 0:S], MULT)
+                else:
+                    nc.vector.tensor_tensor(ad_sb[t][:, 0:S], s1[t][:], y_ps[t][:], MULT)
+            elif i == 3:
+                gather_on(ENG_D[t], s2[t][:], ad_sb[t][:].indirect(d2_sb[:]))
+            elif i == 4:
+                if ENG_E[t] == "G":
+                    nc.gpsimd.tensor_tensor(st[t][:], s2[t][:], ad_sb[t][:, 0:S], ADD)
+                else:
+                    nc.vector.tensor_tensor(st[t][:], s2[t][:], ad_sb[t][:, 0:S], ADD)
+            elif i == 5:
+                nc.scalar.activation(th[t][:], st[t][:], ACT.Tanh)
+            elif i == 6:
+                nc.scalar.activation(ex[t][:], th[t][:], ACT.Exp, scale=1.5, accum_out=tot[t][:])
+            elif i == 7:
+                nc.vector.reciprocal(inv[t][:], tot[t][:])
+            elif i == 8:
+                nc.vector.tensor_scalar(fac[t][:], inv[t][:], unit_s[:, t : t + 1], None, MULT)
+            else:
+                for h in range(2):
+                    cols = slice(h * HALF, (h + 1) * HALF)
+                    nc.vector.scalar_tensor_tensor(hid_pl[h][:, t, :], ex[t][:, cols], fac[t][:], y_ps[t][:, cols], MULT, MULT)
+
+        skew = 1
+        for pos, t, i in sorted((i + skew * t, -t, i) for t in range(PACK) for i in range(10)):
+            step(i, -t)
+
+        w2_bf = keep.tile([P, N, PACK], BF16, name="w2_bf", align_bytes=64)
+        w2_codes = keep.tile([P, N], U32, name="w2_codes", align_bytes=64)
+        w2_scales = keep.tile([P, N], U8, name="w2_scales", align_bytes=64)
+        copy_on("V", w2_bf[:].rearrange("p (c i) j -> p c j i", i=4), w2_raw[:].rearrange("p j (c i) -> p c j i", i=4))
+        nc.vector.quantize_mx(out=w2_codes[:].bitcast(FP8X4), scales=w2_scales[:], in_=w2_bf[:].rearrange("p n j -> p (n j)"))
+
+        for h in range(2):
+            cols = slice(h * HALF, (h + 1) * HALF)
+            hid_bf = keep.tile([P, HALF, PACK], BF16, name="hid_bf%d" % h, align_bytes=64)
+            hid_codes = keep.tile([P, HALF], U32, name="hid_codes%d" % h, align_bytes=64)
+            hid_scales = keep.tile([P, HALF], U8, name="hid_scales%d" % h, align_bytes=64)
+            copy_on("VS"[h], hid_bf[:].rearrange("p (c i) t -> p c t i", i=4), hid_pl[h][:].rearrange("p t (c i) -> p c t i", i=4))
+            nc.vector.quantize_mx(out=hid_codes[:].bitcast(FP8X4), scales=hid_scales[:], in_=hid_bf[:].rearrange("p n j -> p (n j)"))
+            for m in range(N // P):
+                o_ps = psum.tile([P, HALF], F32, name="o_ps%d_%d" % (h, m))
+                nc.tensor.matmul_mx(
+                    out=o_ps[:],
+                    lhsT=w2_codes[:, m * P : (m + 1) * P].bitcast(FP8X4),
+                    lhsT_scale=w2_scales[:, m * P : (m + 1) * P],
+                    rhs=hid_codes[:].bitcast(FP8X4),
+                    rhs_scale=hid_scales[:],
+                    start=True,
+                    stop=True,
+                )
+                o_sb = keep.tile([P, HALF], F32, name="o_sb%d_%d" % (h, m), align_bytes=64)
+                copy_on("SSSV"[2 * h + m], o_sb[:], o_ps[:])
+                nc.sync.dma_start(out=out[m * P : (m + 1) * P, cols], in_=o_sb[:])

@@ -49,9 +49,6 @@ def tile_picked_yanti_val_p_kernel(tc, x_words, x_scales, w1, unit, w2, offs, d1
             nc.vector.memset(ad_sb[t][:, S:WIN], 0.0)
 
         nc.sync.dma_start(offs_sb[:], offs)
-        xs_i32 = x_scales.bitcast(I32)
-        for q in range(4):
-            nc.gpsimd.dma_start(out=xs_all[32 * q : 32 * q + 8, :].bitcast(I32), in_=xs_i32[:, 4 * q : 4 * q + 4, :])
         w1_raw = {}
         xw_all = []
         w1_rows = w1.rearrange("(g p j) c -> g p j c", g=PASSES, j=PACK)
@@ -67,6 +64,9 @@ def tile_picked_yanti_val_p_kernel(tc, x_words, x_scales, w1, unit, w2, offs, d1
             xw_all.append(xw)
 
         load_w1(0, 0, H)
+        xs_i32 = x_scales.bitcast(I32)
+        for q in range(4):
+            nc.sync.dma_start(out=xs_all[32 * q : 32 * q + 8, :].bitcast(I32), in_=xs_i32[:, 4 * q : 4 * q + 4, :])
         load_x(0)
         load_x(1)
         for c0, c1, e in W1_CHUNKS:
@@ -74,15 +74,18 @@ def tile_picked_yanti_val_p_kernel(tc, x_words, x_scales, w1, unit, w2, offs, d1
         nc.sync.dma_start(d1_sb[:], d1)
         nc.sync.dma_start(d2_sb[:], d2)
         unit_sb = keep.tile([P, PACK], F32, name="unit_sb", align_bytes=64)
-        nc.sync.dma_start(out=unit_sb[:], in_=unit.rearrange("(p t) o -> p (t o)", t=PACK))
+        w2_rows = w2.rearrange("(a t i) n -> t a i n", t=PACK, i=4)
         w2_raw = keep.tile([P, PACK, N], F32, name="w2_raw", align_bytes=64)
-        nc.sync.dma_start(out=w2_raw[:], in_=w2.rearrange("(p j) n -> p j n", j=PACK))
+        for t in range(PACK):
+            nc.sync.dma_start(out=w2_raw[:, t, :], in_=w2_rows[t])
+        with nc.allow_non_contiguous_dma(reason="one value a partition"):
+            for i in range(4):
+                nc.sync.dma_start(out=unit_sb[i:P:4, :], in_=unit.rearrange("(a t i) o -> i a (t o)", t=PACK, i=4)[i])
 
         xs = keep.tile([P, S], U8, name="xs", align_bytes=64)
-        nc.vector.tensor_copy(xs[:], xs_all[:].indirect(offs_sb[:]))
         xw = [keep.tile([P, S], U32, name="xw%d" % g, align_bytes=64) for g in range(PASSES)]
 
-        w1_bf = [keep.tile([P, PACK, P, PACK], BF16, name="w1_bf%d" % g, align_bytes=64) for g in range(PASSES)]
+        w1_bf = [[keep.tile([P, P, PACK], BF16, name="w1_bf%d_%d" % (g, t), align_bytes=64) for t in range(PACK)] for g in range(PASSES)]
         w1_codes = [keep.tile([P, H], U32, name="w1_codes%d" % g, align_bytes=64) for g in range(PASSES)]
         w1_scales = [keep.tile([P, H], U8, name="w1_scales%d" % g, align_bytes=64) for g in range(PASSES)]
 
@@ -94,16 +97,17 @@ def tile_picked_yanti_val_p_kernel(tc, x_words, x_scales, w1, unit, w2, offs, d1
             else:
                 nc.vector.tensor_copy(dst, src)
 
-        def cast_w1(g, c0, c1, e):
-            dst = w1_bf[g][:, :, c0 // PACK : c1 // PACK, :].rearrange("p t m j -> p m j t")
-            src = w1_raw[(g, c0)][:].rearrange("p j (m t) -> p m j t", t=PACK)
-            copy_on(e, dst, src)
+        def cast_w1(g, c0, c1):
+            for t in range(PACK):
+                dst = w1_bf[g][t][:, c0 // PACK : c1 // PACK, :].rearrange("p (a i) j -> p a j i", i=4)
+                src = w1_raw[(g, c0)][:].rearrange("p j (a t i) -> p t a j i", t=PACK, i=4)[:, t]
+                copy_on("VVSS"[t], dst, src)
 
-        def quant_w1(g, t0, t1):
+        def quant_w1(g, t):
             nc.vector.quantize_mx(
-                out=w1_codes[g][:, t0 * P : t1 * P].bitcast(FP8X4),
-                scales=w1_scales[g][:, t0 * P : t1 * P],
-                in_=w1_bf[g][:, t0:t1].rearrange("p t m j -> p (t m j)"),
+                out=w1_codes[g][:, t * P : (t + 1) * P].bitcast(FP8X4),
+                scales=w1_scales[g][:, t * P : (t + 1) * P],
+                in_=w1_bf[g][t][:].rearrange("p m j -> p (m j)"),
             )
 
         y_ps = [psum.tile([P, S], F32, name="y_ps%d" % t) for t in range(PACK)]
@@ -119,20 +123,20 @@ def tile_picked_yanti_val_p_kernel(tc, x_words, x_scales, w1, unit, w2, offs, d1
                 stop=(g == PASSES - 1),
             )
 
-        cast_w1(0, 0, H, "S")
-        quant_w1(0, 0, PACK)
+        cast_w1(0, 0, H)
+        for t in range(PACK):
+            quant_w1(0, t)
+        nc.vector.tensor_copy(xs[:], xs_all[:].indirect(offs_sb[:]))
         nc.vector.tensor_copy(xw[0][:], xw_all[0][:].bitcast(U32).indirect(offs_sb[:]))
         for t in range(PACK):
             mm1(0, t)
         nc.vector.tensor_copy(xw[1][:], xw_all[1][:].bitcast(U32).indirect(offs_sb[:]))
         for c0, c1, e in W1_CHUNKS:
-            cast_w1(1, c0, c1, e)
+            cast_w1(1, c0, c1)
         for t in range(PACK):
-            quant_w1(1, t, t + 1)
+            quant_w1(1, t)
             mm1(1, t)
 
-        unit_s = keep.tile([P, PACK], F32, name="unit_s", align_bytes=64)
-        nc.vector.tensor_scalar(unit_s[:], unit_sb[:], float(S), None, MULT)
 
         def gather_on(e, dst, window):
             if e == "S":
@@ -174,7 +178,7 @@ def tile_picked_yanti_val_p_kernel(tc, x_words, x_scales, w1, unit, w2, offs, d1
             elif i == 7:
                 nc.vector.reciprocal(inv[t][:], tot[t][:])
             elif i == 8:
-                nc.vector.tensor_scalar(fac[t][:], inv[t][:], unit_s[:, t : t + 1], None, MULT)
+                nc.vector.tensor_scalar(fac[t][:], inv[t][:], unit_sb[:, t : t + 1], float(S), MULT, MULT)
             else:
                 for h in range(2):
                     cols = slice(h * HALF, (h + 1) * HALF)
@@ -187,7 +191,7 @@ def tile_picked_yanti_val_p_kernel(tc, x_words, x_scales, w1, unit, w2, offs, d1
         w2_bf = keep.tile([P, N, PACK], BF16, name="w2_bf", align_bytes=64)
         w2_codes = keep.tile([P, N], U32, name="w2_codes", align_bytes=64)
         w2_scales = keep.tile([P, N], U8, name="w2_scales", align_bytes=64)
-        copy_on("V", w2_bf[:].rearrange("p (c i) j -> p c j i", i=4), w2_raw[:].rearrange("p j (c i) -> p c j i", i=4))
+        copy_on("S", w2_bf[:].rearrange("p (c i) j -> p c j i", i=4), w2_raw[:].rearrange("p j (c i) -> p c j i", i=4))
         nc.vector.quantize_mx(out=w2_codes[:].bitcast(FP8X4), scales=w2_scales[:], in_=w2_bf[:].rearrange("p n j -> p (n j)"))
 
         for h in range(2):

from contextlib import ExitStack

import concourse.mybir as mybir

K, T, S, N, H = 1024, 2048, 512, 256, 512
FLOPS = 2 * K * H * S + 2 * H * N * S

F32 = mybir.dt.float32
BF16 = mybir.dt.bfloat16
I32 = mybir.dt.int32
U32 = mybir.dt.uint32
U16 = mybir.dt.uint16
U8 = mybir.dt.uint8
FP8X4 = mybir.dt.float8_e4m3fn_x4
MULT = mybir.AluOpType.mult
ADD = mybir.AluOpType.add
ACT = mybir.ActivationFunctionType

P = 128
PACK = 4
PASSES = K // (P * PACK)
WIN = 704
HALF = S // 2
W1_CHUNKS = [(0, 256, "S"), (256, 512, "V")]
ENG_A = "VSVS"
ENG_B = "SVSV"
ENG_C = "VVVV"
ENG_D = "SSVS"
ENG_E = "VVVV"


def tile_picked_yanti_val_p_kernel(tc, x_words, x_scales, w1, unit, w2, offs, d1, d2, out):
    nc = tc.nc
    with ExitStack() as ctx:
        lists = ctx.enter_context(tc.tile_pool(name="lists", bufs=1))
        keep = ctx.enter_context(tc.tile_pool(name="keep", bufs=1))
        psum = ctx.enter_context(tc.psum_pool(name="psum", bufs=1))

        offs_sb = lists.tile([P, S // 16], U16, name="offs_sb")
        d1_sb = lists.tile([P, S // 16], U16, name="d1_sb")
        d2_sb = lists.tile([P, S // 16], U16, name="d2_sb")

        xs_all = keep.tile([P, T], U8, name="xs_all", align_bytes=64)
        nc.gpsimd.memset(xs_all[:].bitcast(I32), 0)
        y_sb = [keep.tile([P, WIN], F32, name="y_sb%d" % t, align_bytes=64) for t in range(PACK)]
        ad_sb = [keep.tile([P, WIN], F32, name="ad_sb%d" % t, align_bytes=64) for t in range(PACK)]
        for t in range(PACK):
            nc.vector.memset(y_sb[t][:, S:WIN], 0.0)
            nc.vector.memset(ad_sb[t][:, S:WIN], 0.0)

        nc.sync.dma_start(offs_sb[:], offs)
        w1_raw = {}
        xw_all = []
        w1_rows = w1.rearrange("(g p j) c -> g p j c", g=PASSES, j=PACK)

        def load_w1(g, c0, c1):
            raw = keep.tile([P, PACK, c1 - c0], F32, name="w1_raw%d_%d" % (g, c0), align_bytes=64)
            nc.sync.dma_start(out=raw[:], in_=w1_rows[g, :, :, c0:c1])
            w1_raw[(g, c0)] = raw

        def load_x(g):
            xw = keep.tile([P, T], I32, name="xw_all%d" % g, align_bytes=64)
            nc.sync.dma_start(out=xw[:], in_=x_words[g].rearrange("p n r -> p (n r)").bitcast(I32))
            xw_all.append(xw)

        load_w1(0, 0, H)
        xs_i32 = x_scales.bitcast(I32)
        for q in range(4):
            nc.sync.dma_start(out=xs_all[32 * q : 32 * q + 8, :].bitcast(I32), in_=xs_i32[:, 4 * q : 4 * q + 4, :])
        load_x(0)
        load_x(1)
        for c0, c1, e in W1_CHUNKS:
            load_w1(1, c0, c1)
        nc.sync.dma_start(d1_sb[:], d1)
        nc.sync.dma_start(d2_sb[:], d2)
        unit_sb = keep.tile([P, PACK], F32, name="unit_sb", align_bytes=64)
        w2_rows = w2.rearrange("(a t i) n -> t a i n", t=PACK, i=4)
        w2_raw = keep.tile([P, PACK, N], F32, name="w2_raw", align_bytes=64)
        for t in range(PACK):
            nc.sync.dma_start(out=w2_raw[:, t, :], in_=w2_rows[t])
        with nc.allow_non_contiguous_dma(reason="one value a partition"):
            for i in range(4):
                nc.sync.dma_start(out=unit_sb[i:P:4, :], in_=unit.rearrange("(a t i) o -> i a (t o)", t=PACK, i=4)[i])

        xs = keep.tile([P, S], U8, name="xs", align_bytes=64)
        xw = [keep.tile([P, S], U32, name="xw%d" % g, align_bytes=64) for g in range(PASSES)]

        w1_bf = [[keep.tile([P, P, PACK], BF16, name="w1_bf%d_%d" % (g, t), align_bytes=64) for t in range(PACK)] for g in range(PASSES)]
        w1_codes = [keep.tile([P, H], U32, name="w1_codes%d" % g, align_bytes=64) for g in range(PASSES)]
        w1_scales = [keep.tile([P, H], U8, name="w1_scales%d" % g, align_bytes=64) for g in range(PASSES)]

        def copy_on(e, dst, src):
            if e == "S":
                nc.scalar.copy(dst, src)
            elif e == "G":
                nc.gpsimd.tensor_copy(dst, src)
            else:
                nc.vector.tensor_copy(dst, src)

        def cast_w1(g, c0, c1):
            for t in range(PACK):
                dst = w1_bf[g][t][:, c0 // PACK : c1 // PACK, :].rearrange("p (a i) j -> p a j i", i=4)
                src = w1_raw[(g, c0)][:].rearrange("p j (a t i) -> p t a j i", t=PACK, i=4)[:, t]
                copy_on("VVSS"[t], dst, src)

        def quant_w1(g, t):
            nc.vector.quantize_mx(
                out=w1_codes[g][:, t * P : (t + 1) * P].bitcast(FP8X4),
                scales=w1_scales[g][:, t * P : (t + 1) * P],
                in_=w1_bf[g][t][:].rearrange("p m j -> p (m j)"),
            )

        y_ps = [psum.tile([P, S], F32, name="y_ps%d" % t) for t in range(PACK)]

        def mm1(g, t):
            nc.tensor.matmul_mx(
                out=y_ps[t][:],
                lhsT=w1_codes[g][:, t * P : (t + 1) * P].bitcast(FP8X4),
                lhsT_scale=w1_scales[g][:, t * P : (t + 1) * P],
                rhs=xw[g][:].bitcast(FP8X4),
                rhs_scale=xs[4 * g : P, :],
                start=(g == 0),
                stop=(g == PASSES - 1),
            )

        cast_w1(0, 0, H)
        for t in range(PACK):
            quant_w1(0, t)
        nc.vector.tensor_copy(xs[:], xs_all[:].indirect(offs_sb[:]))
        nc.vector.tensor_copy(xw[0][:], xw_all[0][:].bitcast(U32).indirect(offs_sb[:]))
        for t in range(PACK):
            mm1(0, t)
        nc.vector.tensor_copy(xw[1][:], xw_all[1][:].bitcast(U32).indirect(offs_sb[:]))
        for c0, c1, e in W1_CHUNKS:
            cast_w1(1, c0, c1)
        for t in range(PACK):
            quant_w1(1, t)
            mm1(1, t)


        def gather_on(e, dst, window):
            if e == "S":
                nc.scalar.activation(dst, window, ACT.Copy)
            else:
                nc.vector.tensor_copy(dst, window)

        s1 = [keep.tile([P, S], F32, name="s1_%d" % t, align_bytes=64) for t in range(PACK)]
        s2 = [keep.tile([P, S], F32, name="s2_%d" % t, align_bytes=64) for t in range(PACK)]
        st = [keep.tile([P, S], F32, name="st%d" % t, align_bytes=64) for t in range(PACK)]
        th = [keep.tile([P, S], F32, name="th%d" % t, align_bytes=64) for t in range(PACK)]
        ex = [keep.tile([P, S], F32, name="ex%d" % t, align_bytes=64) for t in range(PACK)]
        tot = [keep.tile([P, 1], F32, name="tot%d" % t, align_bytes=64) for t in range(PACK)]
        inv = [keep.tile([P, 1], F32, name="inv%d" % t, align_bytes=64) for t in range(PACK)]
        fac = [keep.tile([P, 1], F32, name="fac%d" % t, align_bytes=64) for t in range(PACK)]
        hid_pl = [keep.tile([P, PACK, HALF], BF16, name="hid_pl%d" % h, align_bytes=64) for h in range(2)]

        def step(i, t):
            if i == 0:
                copy_on(ENG_A[t], y_sb[t][:, 0:S], y_ps[t][:])
            elif i == 1:
                gather_on(ENG_B[t], s1[t][:], y_sb[t][:].indirect(d1_sb[:]))
            elif i == 2:
                if ENG_C[t] == "G":
                    nc.gpsimd.tensor_tensor(ad_sb[t][:, 0:S], s1[t][:], y_sb[t][:, 0:S], MULT)
                else:
                    nc.vector.tensor_tensor(ad_sb[t][:, 0:S], s1[t][:], y_ps[t][:], MULT)
            elif i == 3:
                gather_on(ENG_D[t], s2[t][:], ad_sb[t][:].indirect(d2_sb[:]))
            elif i == 4:
                if ENG_E[t] == "G":
                    nc.gpsimd.tensor_tensor(st[t][:], s2[t][:], ad_sb[t][:, 0:S], ADD)
                else:
                    nc.vector.tensor_tensor(st[t][:], s2[t][:], ad_sb[t][:, 0:S], ADD)
            elif i == 5:
                nc.scalar.activation(th[t][:], st[t][:], ACT.Tanh)
            elif i == 6:
                nc.scalar.activation(ex[t][:], th[t][:], ACT.Exp, scale=1.5, accum_out=tot[t][:])
            elif i == 7:
                nc.vector.reciprocal(inv[t][:], tot[t][:])
            elif i == 8:
                nc.vector.tensor_scalar(fac[t][:], inv[t][:], unit_sb[:, t : t + 1], float(S), MULT, MULT)
            else:
                for h in range(2):
                    cols = slice(h * HALF, (h + 1) * HALF)
                    nc.vector.scalar_tensor_tensor(hid_pl[h][:, t, :], ex[t][:, cols], fac[t][:], y_ps[t][:, cols], MULT, MULT)

        skew = 1
        for pos, t, i in sorted((i + skew * t, -t, i) for t in range(PACK) for i in range(10)):
            step(i, -t)

        w2_bf = keep.tile([P, N, PACK], BF16, name="w2_bf", align_bytes=64)
        w2_codes = keep.tile([P, N], U32, name="w2_codes", align_bytes=64)
        w2_scales = keep.tile([P, N], U8, name="w2_scales", align_bytes=64)
        copy_on("S", w2_bf[:].rearrange("p (c i) j -> p c j i", i=4), w2_raw[:].rearrange("p j (c i) -> p c j i", i=4))
        nc.vector.quantize_mx(out=w2_codes[:].bitcast(FP8X4), scales=w2_scales[:], in_=w2_bf[:].rearrange("p n j -> p (n j)"))

        for h in range(2):
            cols = slice(h * HALF, (h + 1) * HALF)
            hid_bf = keep.tile([P, HALF, PACK], BF16, name="hid_bf%d" % h, align_bytes=64)
            hid_codes = keep.tile([P, HALF], U32, name="hid_codes%d" % h, align_bytes=64)
            hid_scales = keep.tile([P, HALF], U8, name="hid_scales%d" % h, align_bytes=64)
            copy_on("VS"[h], hid_bf[:].rearrange("p (c i) t -> p c t i", i=4), hid_pl[h][:].rearrange("p t (c i) -> p c t i", i=4))
            nc.vector.quantize_mx(out=hid_codes[:].bitcast(FP8X4), scales=hid_scales[:], in_=hid_bf[:].rearrange("p n j -> p (n j)"))
            for m in range(N // P):
                o_ps = psum.tile([P, HALF], F32, name="o_ps%d_%d" % (h, m))
                nc.tensor.matmul_mx(
                    out=o_ps[:],
                    lhsT=w2_codes[:, m * P : (m + 1) * P].bitcast(FP8X4),
                    lhsT_scale=w2_scales[:, m * P : (m + 1) * P],
                    rhs=hid_codes[:].bitcast(FP8X4),
                    rhs_scale=hid_scales[:],
                    start=True,
                    stop=True,
                )
                o_sb = keep.tile([P, HALF], F32, name="o_sb%d_%d" % (h, m), align_bytes=64)
                copy_on("SSSV"[2 * h + m], o_sb[:], o_ps[:])
                nc.sync.dma_start(out=out[m * P : (m + 1) * P, cols], in_=o_sb[:])
